import numpy as np
CORES = [2,10,18,26,34,42,50,58,66,74,82,90,98,106,114,122]
N = 16
def setup_inputs(rng):
    return {"x1": rng.standard_normal((N, 128, 64), dtype=np.float32), "x2": rng.standard_normal((N, 128, 1), dtype=np.float32), "x3": rng.standard_normal((N, 128, 256), dtype=np.float32), "x4": rng.standard_normal((N, 128, 16), dtype=np.float32)}
def reference(x1, x2, x3, x4):
    out = {}
    s = x1.sum(axis=0, dtype=np.float64).astype(x1.dtype)
    out["y1"] = np.broadcast_to(s, (N,) + s.shape)
    s = x2.sum(axis=0, dtype=np.float64).astype(x2.dtype)
    out["y2"] = np.broadcast_to(s, (N,) + s.shape)
    s = x3.sum(axis=0, dtype=np.float64).astype(x3.dtype)
    out["y3"] = np.broadcast_to(s, (N,) + s.shape)
    s = x4.sum(axis=0, dtype=np.float64).astype(x4.dtype)
    out["y4"] = np.broadcast_to(s, (N,) + s.shape)
    return out

@@ -1,0 +1,82 @@
+from concourse.bass import DstId, RemoteDMATransfer
+
+WA, WB = 28, 16
+RA = 8 * WA // 2
+
+SCRATCH = {
+    "packA": ("dram", [8, 128, WA], "float32"),
+    "packB": ("dram", [8, 128, WB], "float32"),
+    "landA": ("dram", [16, 128, WA], "float32"),
+    "landB": ("dram", [16, 128, WB], "float32"),
+    "gatA": ("dram", [8, 128, WA], "float32"),
+    "gatB": ("dram", [8, 128, WB], "float32"),
+}
+SEMAPHORES = ["ldA", "ldB", "sent", "inn", "arrA", "arrB", "stored"]
+
+HOST_A = [h for h in range(16) if (h // 2 + h) % 2 == 0]
+HOST_B = [h for h in range(16) if (h // 2 + h) % 2 == 1]
+
+
+def helper_core(h):
+    return 8 * h + (3 if h % 2 == 0 else 7)
+
+
+def dst_id(topo, c):
+    rid, pid, _se = topo.addr(c)
+    return DstId(rid=rid, pnc=pid)
+
+
+def scatter_call(g, core, T, topo, pack, land, hosts, rank):
+    trs = []
+    eng = 0
+    for j, h in enumerate(hosts):
+        hc = helper_core(h)
+        if topo.chip(hc) == topo.chip(core):
+            m = 1 << 8
+        else:
+            m = 1 << eng
+            eng += 1
+        trs.append(RemoteDMATransfer(dst_ids=[dst_id(topo, hc)], dma_engine_mask=m, remote_sem=T.sem.inn,
+                                     src=pack[j], dst=land[rank], alu_op=0))
+    g.remote_dma_fused(trs, local_sem=T.sem.sent)
+
+
+def rank_program(g, core, T, topo):
+    rank = T.rank_of(core)
+    ch = topo.chip(core)
+    if rank is not None:
+        sy, sc = g.sync, g.scalar
+        sy.dma_start(T.packA[:], T.x3[0:RA, :]).then_inc(T.sem.ldA, 16)
+        sc.dma_start(T.packB[2:6], T.x1[:]).then_inc(T.sem.ldB, 16)
+        sy.dma_start(T.packB[0:2], T.x3[RA:128, :]).then_inc(T.sem.ldB, 16)
+        sc.dma_start(T.packB[6], T.x4[:]).then_inc(T.sem.ldB, 16)
+        sy.dma_start(T.packB[7, 0:8, :], T.x2[:]).then_inc(T.sem.ldB, 16)
+        sc.dma_start(T.packB[7, 8:128, :], T.x4[0:120, :]).then_inc(T.sem.ldB, 16)
+        g.wait_ge(T.sem.ldA, 16)
+        scatter_call(g, core, T, topo, T.packA, T.landA, HOST_A, rank)
+        g.wait_ge(T.sem.ldB, 80)
+        scatter_call(g, core, T, topo, T.packB, T.landB, HOST_B, rank)
+        sy.wait_ge(T.sem.arrA, 64)
+        sy.dma_start(T.y3[0:RA, :], T.gatA[:]).then_inc(T.sem.stored, 16)
+        sc.wait_ge(T.sem.arrB, 64)
+        sc.dma_start(T.y1[:], T.gatB[2:6]).then_inc(T.sem.stored, 16)
+        sc.dma_start(T.y2[:], T.gatB[7, 0:8, :]).then_inc(T.sem.stored, 16)
+        sy.wait_ge(T.sem.arrB, 64)
+        sy.dma_start(T.y3[RA:128, :], T.gatB[0:2]).then_inc(T.sem.stored, 16)
+        sy.dma_start(T.y4[:], T.gatB[6]).then_inc(T.sem.stored, 16)
+        g.wait_ge(T.sem.sent, 16)
+        g.wait_ge(T.sem.arrA, 64)
+        g.wait_ge(T.sem.arrB, 64)
+        g.wait_ge(T.sem.stored, 80)
+        return
+    if core != helper_core(ch):
+        return
+    if ch in HOST_A:
+        j, land, gat, arr = HOST_A.index(ch), T.landA, T.gatA, T.sem.arrA
+    else:
+        j, land, gat, arr = HOST_B.index(ch), T.landB, T.gatB, T.sem.arrB
+    g.wait_ge(T.sem.inn, 16)
+    tr = RemoteDMATransfer(dst_ids=[dst_id(topo, c) for c in T.cores], dma_engine_mask=0xFF, remote_sem=arr,
+                           srcs=[land[i] for i in range(16)], dsts=[gat[j] for _c in T.cores], alu_op=1)
+    g.remote_dma_fused([tr], local_sem=T.sem.sent)
+    g.wait_ge(T.sem.sent, 8)

@@ -1,24 +1,30 @@
 from concourse.bass import DstId, RemoteDMATransfer
 
-WA, WB = 28, 16
-RA = 8 * WA // 2
+WIDTH = {"P": 16, "Q": 8, "X": 1}
+COUNT = {"P": 8, "Q": 26, "X": 1}
 
-SCRATCH = {
-    "packA": ("dram", [8, 128, WA], "float32"),
-    "packB": ("dram", [8, 128, WB], "float32"),
-    "landA": ("dram", [16, 128, WA], "float32"),
-    "landB": ("dram", [16, 128, WB], "float32"),
-    "gatA": ("dram", [8, 128, WA], "float32"),
-    "gatB": ("dram", [8, 128, WB], "float32"),
-}
-SEMAPHORES = ["ldA", "ldB", "sent", "inn", "arrA", "arrB", "stored"]
+SCRATCH = {}
+for _c in ("P", "Q", "X"):
+    SCRATCH["pack" + _c] = ("dram", [COUNT[_c], 128, WIDTH[_c]], "float32")
+    SCRATCH["land" + _c] = ("dram", [16, 128, WIDTH[_c]], "float32")
+    SCRATCH["gat" + _c] = ("dram", [COUNT[_c], 128, WIDTH[_c]], "float32")
+SEMAPHORES = ["ld3a", "ld3b", "ldS", "sent", "inn", "arr3a", "arr3b", "arr1", "arr4", "arr2", "stored"]
 
-HOST_A = [h for h in range(16) if (h // 2 + h) % 2 == 0]
-HOST_B = [h for h in range(16) if (h // 2 + h) % 2 == 1]
+CHIPS_A = [h for h in range(16) if (h // 2 + h) % 2 == 0]
+CHIPS_B = [h for h in range(16) if (h // 2 + h) % 2 == 1]
 
-
-def helper_core(h):
-    return 8 * h + (3 if h % 2 == 0 else 7)
+SLOTS = []
+for _j in range(8):
+    SLOTS.append(("P", _j, 8 * CHIPS_A[_j] + 3, "arr3a"))
+for _j in range(8):
+    SLOTS.append(("Q", _j, 8 * CHIPS_B[_j] + 3, "arr3b"))
+for _j in range(8):
+    SLOTS.append(("Q", 8 + _j, 8 * CHIPS_A[_j] + 7, "arr3b"))
+for _j in range(8):
+    SLOTS.append(("Q", 16 + _j, 8 * CHIPS_B[_j] + 7, "arr1"))
+SLOTS.append(("Q", 24, 8 * 1 + 6, "arr4"))
+SLOTS.append(("Q", 25, 8 * 2 + 6, "arr4"))
+SLOTS.append(("X", 0, 8 * 5 + 6, "arr2"))
 
 
 def dst_id(topo, c):
@@ -26,57 +32,70 @@ def dst_id(topo, c):
     return DstId(rid=rid, pnc=pid)
 
 
-def scatter_call(g, core, T, topo, pack, land, hosts, rank):
+def scatter_call(g, core, T, topo, slots, rank):
     trs = []
-    eng = 0
-    for j, h in enumerate(hosts):
-        hc = helper_core(h)
+    off, on = 0, 8
+    for cls, j, hc, _arr in slots:
         if topo.chip(hc) == topo.chip(core):
-            m = 1 << 8
+            m = 1 << on
+            on += 1
         else:
-            m = 1 << eng
-            eng += 1
+            m = 1 << off
+            off += 1
         trs.append(RemoteDMATransfer(dst_ids=[dst_id(topo, hc)], dma_engine_mask=m, remote_sem=T.sem.inn,
-                                     src=pack[j], dst=land[rank], alu_op=0))
+                                     src=T["pack" + cls][j], dst=T["land" + cls][rank], alu_op=0))
     g.remote_dma_fused(trs, local_sem=T.sem.sent)
 
 
 def rank_program(g, core, T, topo):
     rank = T.rank_of(core)
-    ch = topo.chip(core)
     if rank is not None:
         sy, sc = g.sync, g.scalar
-        sy.dma_start(T.packA[:], T.x3[0:RA, :]).then_inc(T.sem.ldA, 16)
-        sc.dma_start(T.packB[2:6], T.x1[:]).then_inc(T.sem.ldB, 16)
-        sy.dma_start(T.packB[0:2], T.x3[RA:128, :]).then_inc(T.sem.ldB, 16)
-        sc.dma_start(T.packB[6], T.x4[:]).then_inc(T.sem.ldB, 16)
-        sy.dma_start(T.packB[7, 0:8, :], T.x2[:]).then_inc(T.sem.ldB, 16)
-        sc.dma_start(T.packB[7, 8:128, :], T.x4[0:120, :]).then_inc(T.sem.ldB, 16)
-        g.wait_ge(T.sem.ldA, 16)
-        scatter_call(g, core, T, topo, T.packA, T.landA, HOST_A, rank)
-        g.wait_ge(T.sem.ldB, 80)
-        scatter_call(g, core, T, topo, T.packB, T.landB, HOST_B, rank)
-        sy.wait_ge(T.sem.arrA, 64)
-        sy.dma_start(T.y3[0:RA, :], T.gatA[:]).then_inc(T.sem.stored, 16)
-        sc.wait_ge(T.sem.arrB, 64)
-        sc.dma_start(T.y1[:], T.gatB[2:6]).then_inc(T.sem.stored, 16)
-        sc.dma_start(T.y2[:], T.gatB[7, 0:8, :]).then_inc(T.sem.stored, 16)
-        sy.wait_ge(T.sem.arrB, 64)
-        sy.dma_start(T.y3[RA:128, :], T.gatB[0:2]).then_inc(T.sem.stored, 16)
-        sy.dma_start(T.y4[:], T.gatB[6]).then_inc(T.sem.stored, 16)
-        g.wait_ge(T.sem.sent, 16)
-        g.wait_ge(T.sem.arrA, 64)
-        g.wait_ge(T.sem.arrB, 64)
+        sy.dma_start(T.packP[:], T.x3[0:64, :]).then_inc(T.sem.ld3a, 16)
+        sc.dma_start(T.packQ[0:16], T.x3[64:128, :]).then_inc(T.sem.ld3b, 16)
+        sy.dma_start(T.packQ[16:24], T.x1[:]).then_inc(T.sem.ldS, 16)
+        sc.dma_start(T.packQ[24:26], T.x4[:]).then_inc(T.sem.ldS, 16)
+        sy.dma_start(T.packX[0], T.x2[:]).then_inc(T.sem.ldS, 16)
+        g.wait_ge(T.sem.ld3a, 16)
+        scatter_call(g, core, T, topo, SLOTS[0:8], rank)
+        g.wait_ge(T.sem.ld3b, 16)
+        scatter_call(g, core, T, topo, SLOTS[8:16], rank)
+        scatter_call(g, core, T, topo, SLOTS[16:24], rank)
+        g.wait_ge(T.sem.ldS, 48)
+        scatter_call(g, core, T, topo, SLOTS[24:32], rank)
+        scatter_call(g, core, T, topo, SLOTS[32:34], rank)
+        scatter_call(g, core, T, topo, SLOTS[34:35], rank)
+        sy.wait_ge(T.sem.arr3a, 64)
+        sy.dma_start(T.y3[0:64, :], T.gatP[:]).then_inc(T.sem.stored, 16)
+        sy.wait_ge(T.sem.arr3b, 128)
+        sy.dma_start(T.y3[64:128, :], T.gatQ[0:16]).then_inc(T.sem.stored, 16)
+        sc.wait_ge(T.sem.arr1, 64)
+        sc.dma_start(T.y1[:], T.gatQ[16:24]).then_inc(T.sem.stored, 16)
+        sc.wait_ge(T.sem.arr4, 16)
+        sc.dma_start(T.y4[:], T.gatQ[24:26]).then_inc(T.sem.stored, 16)
+        sy.wait_ge(T.sem.arr2, 1)
+        sy.dma_start(T.y2[:], T.gatX[0]).then_inc(T.sem.stored, 16)
+        g.wait_ge(T.sem.sent, 35)
+        g.wait_ge(T.sem.arr3a, 64)
+        g.wait_ge(T.sem.arr3b, 128)
+        g.wait_ge(T.sem.arr1, 64)
+        g.wait_ge(T.sem.arr4, 16)
+        g.wait_ge(T.sem.arr2, 1)
         g.wait_ge(T.sem.stored, 80)
         return
-    if core != helper_core(ch):
+    mine = [s for s in SLOTS if s[2] == core]
+    if not mine:
         return
-    if ch in HOST_A:
-        j, land, gat, arr = HOST_A.index(ch), T.landA, T.gatA, T.sem.arrA
-    else:
-        j, land, gat, arr = HOST_B.index(ch), T.landB, T.gatB, T.sem.arrB
+    cls, j, _hc, arr = mine[0]
+    land, gat = T["land" + cls], T["gat" + cls]
+    parts = 8 if cls == "X" else 1
+    ne, nd = 8 // parts, 16 // parts
     g.wait_ge(T.sem.inn, 16)
-    tr = RemoteDMATransfer(dst_ids=[dst_id(topo, c) for c in T.cores], dma_engine_mask=0xFF, remote_sem=arr,
-                           srcs=[land[i] for i in range(16)], dsts=[gat[j] for _c in T.cores], alu_op=1)
-    g.remote_dma_fused([tr], local_sem=T.sem.sent)
+    trs = []
+    for p in range(parts):
+        cs = T.cores[p * nd:(p + 1) * nd]
+        trs.append(RemoteDMATransfer(dst_ids=[dst_id(topo, c) for c in cs],
+                                     dma_engine_mask=((1 << ne) - 1) << (p * ne), remote_sem=T.sem[arr],
+                                     srcs=[land[i] for i in range(16)], dsts=[gat[j] for _c in cs], alu_op=1))
+    g.remote_dma_fused(trs, local_sem=T.sem.sent)
     g.wait_ge(T.sem.sent, 8)

@@ -1,30 +1,24 @@
 from concourse.bass import DstId, RemoteDMATransfer
 
-WIDTH = {"P": 16, "Q": 8, "X": 1}
-COUNT = {"P": 8, "Q": 26, "X": 1}
-
-SCRATCH = {}
-for _c in ("P", "Q", "X"):
-    SCRATCH["pack" + _c] = ("dram", [COUNT[_c], 128, WIDTH[_c]], "float32")
-    SCRATCH["land" + _c] = ("dram", [16, 128, WIDTH[_c]], "float32")
-    SCRATCH["gat" + _c] = ("dram", [COUNT[_c], 128, WIDTH[_c]], "float32")
-SEMAPHORES = ["ld3a", "ld3b", "ldS", "sent", "inn", "arr3a", "arr3b", "arr1", "arr4", "arr2", "stored"]
-
 CHIPS_A = [h for h in range(16) if (h // 2 + h) % 2 == 0]
 CHIPS_B = [h for h in range(16) if (h // 2 + h) % 2 == 1]
 
-SLOTS = []
-for _j in range(8):
-    SLOTS.append(("P", _j, 8 * CHIPS_A[_j] + 3, "arr3a"))
-for _j in range(8):
-    SLOTS.append(("Q", _j, 8 * CHIPS_B[_j] + 3, "arr3b"))
-for _j in range(8):
-    SLOTS.append(("Q", 8 + _j, 8 * CHIPS_A[_j] + 7, "arr3b"))
-for _j in range(8):
-    SLOTS.append(("Q", 16 + _j, 8 * CHIPS_B[_j] + 7, "arr1"))
-SLOTS.append(("Q", 24, 8 * 1 + 6, "arr4"))
-SLOTS.append(("Q", 25, 8 * 2 + 6, "arr4"))
-SLOTS.append(("X", 0, 8 * 5 + 6, "arr2"))
+CLASSES = [
+    ("U", 14, [8 * h + 3 for h in CHIPS_A]),
+    ("V", 12, [8 * h + 7 for h in CHIPS_B]),
+    ("Q", 8, [8 * h + 3 for h in CHIPS_B]),
+    ("W", 6, [8 * h + 7 for h in CHIPS_A]),
+    ("R", 4, [8 * h + 6 for h in (0, 3, 5, 6)]),
+    ("X", 1, [8 * 9 + 6]),
+]
+
+SCRATCH = {}
+SEMAPHORES = ["ldU", "ldV", "ldS", "sent", "inn", "stored"]
+for _c, _w, _hs in CLASSES:
+    SCRATCH["pack" + _c] = ("dram", [len(_hs), 128, _w], "float32")
+    SCRATCH["land" + _c] = ("dram", [16, 128, _w], "float32")
+    SCRATCH["gat" + _c] = ("dram", [len(_hs), 128, _w], "float32")
+    SEMAPHORES.append("arr" + _c)
 
 
 def dst_id(topo, c):
@@ -32,10 +26,11 @@ def dst_id(topo, c):
     return DstId(rid=rid, pnc=pid)
 
 
-def scatter_call(g, core, T, topo, slots, rank):
+def scatter_call(g, core, T, topo, k, rank):
+    cls, _w, helpers = CLASSES[k]
     trs = []
     off, on = 0, 8
-    for cls, j, hc, _arr in slots:
+    for j, hc in enumerate(helpers):
         if topo.chip(hc) == topo.chip(core):
             m = 1 << on
             on += 1
@@ -51,42 +46,40 @@ def rank_program(g, core, T, topo):
     rank = T.rank_of(core)
     if rank is not None:
         sy, sc = g.sync, g.scalar
-        sy.dma_start(T.packP[:], T.x3[0:64, :]).then_inc(T.sem.ld3a, 16)
-        sc.dma_start(T.packQ[0:16], T.x3[64:128, :]).then_inc(T.sem.ld3b, 16)
-        sy.dma_start(T.packQ[16:24], T.x1[:]).then_inc(T.sem.ldS, 16)
-        sc.dma_start(T.packQ[24:26], T.x4[:]).then_inc(T.sem.ldS, 16)
-        sy.dma_start(T.packX[0], T.x2[:]).then_inc(T.sem.ldS, 16)
-        g.wait_ge(T.sem.ld3a, 16)
-        scatter_call(g, core, T, topo, SLOTS[0:8], rank)
-        g.wait_ge(T.sem.ld3b, 16)
-        scatter_call(g, core, T, topo, SLOTS[8:16], rank)
-        scatter_call(g, core, T, topo, SLOTS[16:24], rank)
-        g.wait_ge(T.sem.ldS, 48)
-        scatter_call(g, core, T, topo, SLOTS[24:32], rank)
-        scatter_call(g, core, T, topo, SLOTS[32:34], rank)
-        scatter_call(g, core, T, topo, SLOTS[34:35], rank)
-        sy.wait_ge(T.sem.arr3a, 64)
-        sy.dma_start(T.y3[0:64, :], T.gatP[:]).then_inc(T.sem.stored, 16)
-        sy.wait_ge(T.sem.arr3b, 128)
-        sy.dma_start(T.y3[64:128, :], T.gatQ[0:16]).then_inc(T.sem.stored, 16)
-        sc.wait_ge(T.sem.arr1, 64)
-        sc.dma_start(T.y1[:], T.gatQ[16:24]).then_inc(T.sem.stored, 16)
-        sc.wait_ge(T.sem.arr4, 16)
-        sc.dma_start(T.y4[:], T.gatQ[24:26]).then_inc(T.sem.stored, 16)
-        sy.wait_ge(T.sem.arr2, 1)
+        sy.dma_start(T.packU[:], T.x3[0:56, :]).then_inc(T.sem.ldU, 16)
+        sc.dma_start(T.packV[:], T.x3[56:104, :]).then_inc(T.sem.ldV, 16)
+        sy.dma_start(T.packQ[:], T.x1[:]).then_inc(T.sem.ldS, 16)
+        sc.dma_start(T.packW[:], T.x3[104:128, :]).then_inc(T.sem.ldS, 16)
+        sy.dma_start(T.packR[:], T.x4[:]).then_inc(T.sem.ldS, 16)
+        sc.dma_start(T.packX[0], T.x2[:]).then_inc(T.sem.ldS, 16)
+        g.wait_ge(T.sem.ldU, 16)
+        scatter_call(g, core, T, topo, 0, rank)
+        g.wait_ge(T.sem.ldV, 16)
+        scatter_call(g, core, T, topo, 1, rank)
+        g.wait_ge(T.sem.ldS, 64)
+        for k in range(2, 6):
+            scatter_call(g, core, T, topo, k, rank)
+        sy.wait_ge(T.sem.arrU, 64)
+        sy.dma_start(T.y3[0:56, :], T.gatU[:]).then_inc(T.sem.stored, 16)
+        sc.wait_ge(T.sem.arrV, 64)
+        sc.dma_start(T.y3[56:104, :], T.gatV[:]).then_inc(T.sem.stored, 16)
+        sc.wait_ge(T.sem.arrQ, 64)
+        sc.dma_start(T.y1[:], T.gatQ[:]).then_inc(T.sem.stored, 16)
+        sy.wait_ge(T.sem.arrW, 64)
+        sy.dma_start(T.y3[104:128, :], T.gatW[:]).then_inc(T.sem.stored, 16)
+        sc.wait_ge(T.sem.arrR, 32)
+        sc.dma_start(T.y4[:], T.gatR[:]).then_inc(T.sem.stored, 16)
+        sy.wait_ge(T.sem.arrX, 1)
         sy.dma_start(T.y2[:], T.gatX[0]).then_inc(T.sem.stored, 16)
-        g.wait_ge(T.sem.sent, 35)
-        g.wait_ge(T.sem.arr3a, 64)
-        g.wait_ge(T.sem.arr3b, 128)
-        g.wait_ge(T.sem.arr1, 64)
-        g.wait_ge(T.sem.arr4, 16)
-        g.wait_ge(T.sem.arr2, 1)
-        g.wait_ge(T.sem.stored, 80)
+        g.wait_ge(T.sem.sent, 37)
+        for cls, n in (("U", 64), ("V", 64), ("Q", 64), ("W", 64), ("R", 32), ("X", 1)):
+            g.wait_ge(T.sem["arr" + cls], n)
+        g.wait_ge(T.sem.stored, 96)
         return
-    mine = [s for s in SLOTS if s[2] == core]
+    mine = [(cls, hs.index(core)) for cls, _w, hs in CLASSES if core in hs]
     if not mine:
         return
-    cls, j, _hc, arr = mine[0]
+    cls, j = mine[0]
     land, gat = T["land" + cls], T["gat" + cls]
     parts = 8 if cls == "X" else 1
     ne, nd = 8 // parts, 16 // parts
@@ -95,7 +88,7 @@ def rank_program(g, core, T, topo):
     for p in range(parts):
         cs = T.cores[p * nd:(p + 1) * nd]
         trs.append(RemoteDMATransfer(dst_ids=[dst_id(topo, c) for c in cs],
-                                     dma_engine_mask=((1 << ne) - 1) << (p * ne), remote_sem=T.sem[arr],
+                                     dma_engine_mask=((1 << ne) - 1) << (p * ne), remote_sem=T.sem["arr" + cls],
                                      srcs=[land[i] for i in range(16)], dsts=[gat[j] for _c in cs], alu_op=1))
     g.remote_dma_fused(trs, local_sem=T.sem.sent)
     g.wait_ge(T.sem.sent, 8)

@@ -11,6 +11,8 @@ CLASSES = [
     ("R", 4, [8 * h + 6 for h in (0, 3, 5, 6)]),
     ("X", 1, [8 * 9 + 6]),
 ]
+PARTS = {"U": 2, "V": 2, "Q": 2, "W": 2, "R": 2, "X": 8}
+ARRIVED = {}
 
 SCRATCH = {}
 SEMAPHORES = ["ldU", "ldV", "ldS", "sent", "inn", "stored"]
@@ -19,6 +21,7 @@ for _c, _w, _hs in CLASSES:
     SCRATCH["land" + _c] = ("dram", [16, 128, _w], "float32")
     SCRATCH["gat" + _c] = ("dram", [len(_hs), 128, _w], "float32")
     SEMAPHORES.append("arr" + _c)
+    ARRIVED[_c] = len(_hs) * (8 // PARTS[_c])
 
 
 def dst_id(topo, c):
@@ -59,21 +62,21 @@ def rank_program(g, core, T, topo):
         g.wait_ge(T.sem.ldS, 64)
         for k in range(2, 6):
             scatter_call(g, core, T, topo, k, rank)
-        sy.wait_ge(T.sem.arrU, 64)
+        sy.wait_ge(T.sem.arrU, ARRIVED["U"])
         sy.dma_start(T.y3[0:56, :], T.gatU[:]).then_inc(T.sem.stored, 16)
-        sc.wait_ge(T.sem.arrV, 64)
+        sc.wait_ge(T.sem.arrV, ARRIVED["V"])
         sc.dma_start(T.y3[56:104, :], T.gatV[:]).then_inc(T.sem.stored, 16)
-        sc.wait_ge(T.sem.arrQ, 64)
+        sc.wait_ge(T.sem.arrQ, ARRIVED["Q"])
         sc.dma_start(T.y1[:], T.gatQ[:]).then_inc(T.sem.stored, 16)
-        sy.wait_ge(T.sem.arrW, 64)
+        sy.wait_ge(T.sem.arrW, ARRIVED["W"])
         sy.dma_start(T.y3[104:128, :], T.gatW[:]).then_inc(T.sem.stored, 16)
-        sc.wait_ge(T.sem.arrR, 32)
+        sc.wait_ge(T.sem.arrR, ARRIVED["R"])
         sc.dma_start(T.y4[:], T.gatR[:]).then_inc(T.sem.stored, 16)
-        sy.wait_ge(T.sem.arrX, 1)
+        sy.wait_ge(T.sem.arrX, ARRIVED["X"])
         sy.dma_start(T.y2[:], T.gatX[0]).then_inc(T.sem.stored, 16)
         g.wait_ge(T.sem.sent, 37)
-        for cls, n in (("U", 64), ("V", 64), ("Q", 64), ("W", 64), ("R", 32), ("X", 1)):
-            g.wait_ge(T.sem["arr" + cls], n)
+        for cls, _w, _hs in CLASSES:
+            g.wait_ge(T.sem["arr" + cls], ARRIVED[cls])
         g.wait_ge(T.sem.stored, 96)
         return
     mine = [(cls, hs.index(core)) for cls, _w, hs in CLASSES if core in hs]
@@ -81,7 +84,7 @@ def rank_program(g, core, T, topo):
         return
     cls, j = mine[0]
     land, gat = T["land" + cls], T["gat" + cls]
-    parts = 8 if cls == "X" else 1
+    parts = PARTS[cls]
     ne, nd = 8 // parts, 16 // parts
     g.wait_ge(T.sem.inn, 16)
     trs = []

@@ -4,24 +4,26 @@ CHIPS_A = [h for h in range(16) if (h // 2 + h) % 2 == 0]
 CHIPS_B = [h for h in range(16) if (h // 2 + h) % 2 == 1]
 
 CLASSES = [
-    ("U", 14, [8 * h + 3 for h in CHIPS_A]),
+    ("U", 12, [8 * h + 3 for h in CHIPS_A]),
     ("V", 12, [8 * h + 7 for h in CHIPS_B]),
     ("Q", 8, [8 * h + 3 for h in CHIPS_B]),
-    ("W", 6, [8 * h + 7 for h in CHIPS_A]),
-    ("R", 4, [8 * h + 6 for h in (0, 3, 5, 6)]),
-    ("X", 1, [8 * 9 + 6]),
+    ("W", 8, [8 * h + 7 for h in CHIPS_A]),
+    ("R", 4, [8 * h + 6 for h in (0, 3, 5, 6, 9)]),
 ]
-PARTS = {"U": 2, "V": 2, "Q": 2, "W": 2, "R": 2, "X": 8}
-ARRIVED = {}
+RU, RV = 48, 96
+PARTS = 2
+PACK_ROW = {c: [128 * j for j in range(len(hs))] for c, _w, hs in CLASSES}
+PACK_ROW["R"][4] = 512 + 32 - 128
+PACK_ROWS = {c: PACK_ROW[c][-1] + 128 for c, _w, hs in CLASSES}
+ARRIVED = {c: len(hs) * (8 // PARTS) for c, _w, hs in CLASSES}
 
 SCRATCH = {}
 SEMAPHORES = ["ldU", "ldV", "ldS", "sent", "inn", "stored"]
 for _c, _w, _hs in CLASSES:
-    SCRATCH["pack" + _c] = ("dram", [len(_hs), 128, _w], "float32")
+    SCRATCH["pack" + _c] = ("dram", [PACK_ROWS[_c], _w], "float32")
     SCRATCH["land" + _c] = ("dram", [16, 128, _w], "float32")
     SCRATCH["gat" + _c] = ("dram", [len(_hs), 128, _w], "float32")
     SEMAPHORES.append("arr" + _c)
-    ARRIVED[_c] = len(_hs) * (8 // PARTS[_c])
 
 
 def dst_id(topo, c):
@@ -40,8 +42,9 @@ def scatter_call(g, core, T, topo, k, rank):
         else:
             m = 1 << off
             off += 1
+        r0 = PACK_ROW[cls][j]
         trs.append(RemoteDMATransfer(dst_ids=[dst_id(topo, hc)], dma_engine_mask=m, remote_sem=T.sem.inn,
-                                     src=T["pack" + cls][j], dst=T["land" + cls][rank], alu_op=0))
+                                     src=T["pack" + cls][r0:r0 + 128, :], dst=T["land" + cls][rank], alu_op=0))
     g.remote_dma_fused(trs, local_sem=T.sem.sent)
 
 
@@ -49,31 +52,31 @@ def rank_program(g, core, T, topo):
     rank = T.rank_of(core)
     if rank is not None:
         sy, sc = g.sync, g.scalar
-        sy.dma_start(T.packU[:], T.x3[0:56, :]).then_inc(T.sem.ldU, 16)
-        sc.dma_start(T.packV[:], T.x3[56:104, :]).then_inc(T.sem.ldV, 16)
+        sy.dma_start(T.packU[:], T.x3[0:RU, :]).then_inc(T.sem.ldU, 16)
+        sc.dma_start(T.packV[:], T.x3[RU:RV, :]).then_inc(T.sem.ldV, 16)
         sy.dma_start(T.packQ[:], T.x1[:]).then_inc(T.sem.ldS, 16)
-        sc.dma_start(T.packW[:], T.x3[104:128, :]).then_inc(T.sem.ldS, 16)
-        sy.dma_start(T.packR[:], T.x4[:]).then_inc(T.sem.ldS, 16)
-        sc.dma_start(T.packX[0], T.x2[:]).then_inc(T.sem.ldS, 16)
+        sc.dma_start(T.packW[:], T.x3[RV:128, :]).then_inc(T.sem.ldS, 16)
+        sy.dma_start(T.packR[0:512, :], T.x4[:]).then_inc(T.sem.ldS, 16)
+        sc.dma_start(T.packR[512:544, :], T.x2[:]).then_inc(T.sem.ldS, 16)
         g.wait_ge(T.sem.ldU, 16)
         scatter_call(g, core, T, topo, 0, rank)
         g.wait_ge(T.sem.ldV, 16)
         scatter_call(g, core, T, topo, 1, rank)
         g.wait_ge(T.sem.ldS, 64)
-        for k in range(2, 6):
+        for k in range(2, 5):
             scatter_call(g, core, T, topo, k, rank)
         sy.wait_ge(T.sem.arrU, ARRIVED["U"])
-        sy.dma_start(T.y3[0:56, :], T.gatU[:]).then_inc(T.sem.stored, 16)
+        sy.dma_start(T.y3[0:RU, :], T.gatU[:]).then_inc(T.sem.stored, 16)
         sc.wait_ge(T.sem.arrV, ARRIVED["V"])
-        sc.dma_start(T.y3[56:104, :], T.gatV[:]).then_inc(T.sem.stored, 16)
+        sc.dma_start(T.y3[RU:RV, :], T.gatV[:]).then_inc(T.sem.stored, 16)
         sc.wait_ge(T.sem.arrQ, ARRIVED["Q"])
         sc.dma_start(T.y1[:], T.gatQ[:]).then_inc(T.sem.stored, 16)
         sy.wait_ge(T.sem.arrW, ARRIVED["W"])
-        sy.dma_start(T.y3[104:128, :], T.gatW[:]).then_inc(T.sem.stored, 16)
+        sy.dma_start(T.y3[RV:128, :], T.gatW[:]).then_inc(T.sem.stored, 16)
         sc.wait_ge(T.sem.arrR, ARRIVED["R"])
-        sc.dma_start(T.y4[:], T.gatR[:]).then_inc(T.sem.stored, 16)
-        sy.wait_ge(T.sem.arrX, ARRIVED["X"])
-        sy.dma_start(T.y2[:], T.gatX[0]).then_inc(T.sem.stored, 16)
+        sc.dma_start(T.y4[:], T.gatR[0:4]).then_inc(T.sem.stored, 16)
+        sy.wait_ge(T.sem.arrR, ARRIVED["R"])
+        sy.dma_start(T.y2[:], T.gatR[4, 96:128, :]).then_inc(T.sem.stored, 16)
         g.wait_ge(T.sem.sent, 37)
         for cls, _w, _hs in CLASSES:
             g.wait_ge(T.sem["arr" + cls], ARRIVED[cls])
@@ -84,11 +87,10 @@ def rank_program(g, core, T, topo):
         return
     cls, j = mine[0]
     land, gat = T["land" + cls], T["gat" + cls]
-    parts = PARTS[cls]
-    ne, nd = 8 // parts, 16 // parts
+    ne, nd = 8 // PARTS, 16 // PARTS
     g.wait_ge(T.sem.inn, 16)
     trs = []
-    for p in range(parts):
+    for p in range(PARTS):
         cs = T.cores[p * nd:(p + 1) * nd]
         trs.append(RemoteDMATransfer(dst_ids=[dst_id(topo, c) for c in cs],
                                      dma_engine_mask=((1 << ne) - 1) << (p * ne), remote_sem=T.sem["arr" + cls],

from concourse.bass import DstId, RemoteDMATransfer

CHIPS_A = [h for h in range(16) if (h // 2 + h) % 2 == 0]
CHIPS_B = [h for h in range(16) if (h // 2 + h) % 2 == 1]

CLASSES = [
    ("U", 12, [8 * h + 3 for h in CHIPS_A]),
    ("V", 12, [8 * h + 7 for h in CHIPS_B]),
    ("Q", 8, [8 * h + 3 for h in CHIPS_B]),
    ("W", 8, [8 * h + 7 for h in CHIPS_A]),
    ("R", 4, [8 * h + 6 for h in (0, 3, 5, 6, 9)]),
]
RU, RV = 48, 96
PARTS = 2
PACK_ROW = {c: [128 * j for j in range(len(hs))] for c, _w, hs in CLASSES}
PACK_ROW["R"][4] = 512 + 32 - 128
PACK_ROWS = {c: PACK_ROW[c][-1] + 128 for c, _w, hs in CLASSES}
ARRIVED = {c: len(hs) * (8 // PARTS) for c, _w, hs in CLASSES}

SCRATCH = {}
SEMAPHORES = ["ldU", "ldV", "ldS", "sent", "inn", "stored"]
for _c, _w, _hs in CLASSES:
    SCRATCH["pack" + _c] = ("dram", [PACK_ROWS[_c], _w], "float32")
    SCRATCH["land" + _c] = ("dram", [16, 128, _w], "float32")
    SCRATCH["gat" + _c] = ("dram", [len(_hs), 128, _w], "float32")
    SEMAPHORES.append("arr" + _c)


def dst_id(topo, c):
    rid, pid, _se = topo.addr(c)
    return DstId(rid=rid, pnc=pid)


def scatter_call(g, core, T, topo, k, rank):
    cls, _w, helpers = CLASSES[k]
    trs = []
    off, on = 0, 8
    for j, hc in enumerate(helpers):
        if topo.chip(hc) == topo.chip(core):
            m = 1 << on
            on += 1
        else:
            m = 1 << off
            off += 1
        r0 = PACK_ROW[cls][j]
        trs.append(RemoteDMATransfer(dst_ids=[dst_id(topo, hc)], dma_engine_mask=m, remote_sem=T.sem.inn,
                                     src=T["pack" + cls][r0:r0 + 128, :], dst=T["land" + cls][rank], alu_op=0))
    g.remote_dma_fused(trs, local_sem=T.sem.sent)


def rank_program(g, core, T, topo):
    rank = T.rank_of(core)
    if rank is not None:
        sy, sc = g.sync, g.scalar
        sy.dma_start(T.packU[:], T.x3[0:RU, :]).then_inc(T.sem.ldU, 16)
        sc.dma_start(T.packV[:], T.x3[RU:RV, :]).then_inc(T.sem.ldV, 16)
        sy.dma_start(T.packQ[:], T.x1[:]).then_inc(T.sem.ldS, 16)
        sc.dma_start(T.packW[:], T.x3[RV:128, :]).then_inc(T.sem.ldS, 16)
        sy.dma_start(T.packR[0:512, :], T.x4[:]).then_inc(T.sem.ldS, 16)
        sc.dma_start(T.packR[512:544, :], T.x2[:]).then_inc(T.sem.ldS, 16)
        g.wait_ge(T.sem.ldU, 16)
        scatter_call(g, core, T, topo, 0, rank)
        g.wait_ge(T.sem.ldV, 16)
        scatter_call(g, core, T, topo, 1, rank)
        g.wait_ge(T.sem.ldS, 64)
        for k in range(2, 5):
            scatter_call(g, core, T, topo, k, rank)
        sy.wait_ge(T.sem.arrU, ARRIVED["U"])
        sy.dma_start(T.y3[0:RU, :], T.gatU[:]).then_inc(T.sem.stored, 16)
        sc.wait_ge(T.sem.arrV, ARRIVED["V"])
        sc.dma_start(T.y3[RU:RV, :], T.gatV[:]).then_inc(T.sem.stored, 16)
        sc.wait_ge(T.sem.arrQ, ARRIVED["Q"])
        sc.dma_start(T.y1[:], T.gatQ[:]).then_inc(T.sem.stored, 16)
        sy.wait_ge(T.sem.arrW, ARRIVED["W"])
        sy.dma_start(T.y3[RV:128, :], T.gatW[:]).then_inc(T.sem.stored, 16)
        sc.wait_ge(T.sem.arrR, ARRIVED["R"])
        sc.dma_start(T.y4[:], T.gatR[0:4]).then_inc(T.sem.stored, 16)
        sy.wait_ge(T.sem.arrR, ARRIVED["R"])
        sy.dma_start(T.y2[:], T.gatR[4, 96:128, :]).then_inc(T.sem.stored, 16)
        g.wait_ge(T.sem.sent, 37)
        for cls, _w, _hs in CLASSES:
            g.wait_ge(T.sem["arr" + cls], ARRIVED[cls])
        g.wait_ge(T.sem.stored, 96)
        return
    mine = [(cls, hs.index(core)) for cls, _w, hs in CLASSES if core in hs]
    if not mine:
        return
    cls, j = mine[0]
    land, gat = T["land" + cls], T["gat" + cls]
    ne, nd = 8 // PARTS, 16 // PARTS
    g.wait_ge(T.sem.inn, 16)
    trs = []
    for p in range(PARTS):
        cs = T.cores[p * nd:(p + 1) * nd]
        trs.append(RemoteDMATransfer(dst_ids=[dst_id(topo, c) for c in cs],
                                     dma_engine_mask=((1 << ne) - 1) << (p * ne), remote_sem=T.sem["arr" + cls],
                                     srcs=[land[i] for i in range(16)], dsts=[gat[j] for _c in cs], alu_op=1))
    g.remote_dma_fused(trs, local_sem=T.sem.sent)
    g.wait_ge(T.sem.sent, 8)
